import numpy as np
import ml_dtypes


def mxq(x, axis, fmt="e4m3"):
    dtype, down = {"e4m3": (ml_dtypes.float8_e4m3fn, 7), "e5m2": (ml_dtypes.float8_e5m2, 14)}[fmt]
    v = np.moveaxis(np.asarray(x, np.float32).astype(ml_dtypes.bfloat16).astype(np.float64), axis, -1)
    blocks = v.reshape(v.shape[:-1] + (-1, 32))
    amax = np.abs(blocks).max(-1, keepdims=True)
    byte = np.maximum(np.where(amax > 0, np.frexp(amax)[1] - 1 + 127, 0) - down, 1)
    scale = np.exp2(byte - 127.0)
    codes = (blocks / scale).astype(np.float32).astype(dtype).astype(np.float64)
    return np.moveaxis((codes * scale).reshape(v.shape), -1, axis)


WIDE = False


def mx_kscale(k):
    if not WIDE:
        return np.ones(k)
    levels = np.array([10, -10, 5, -5, 0])
    if k % 512:
        return np.exp2(np.random.permutation(np.resize(levels, k // 32))).repeat(32)
    a = np.empty((k // 512, 16))
    for p in range(k // 512):
        a[p, :8] = np.random.permutation(np.resize(levels, 8))
        for g in range(8):
            far = levels[np.abs(levels - a[p, g]) >= 10]
            a[p, g + 8] = far[np.random.randint(len(far))]
    return np.exp2(a.ravel()).repeat(32)


def f64(x):
    return np.asarray(x).astype(np.float64)


def striped(idx):
    return np.tile(np.asarray(idx).reshape(-1, 16).T, (8, 1)).astype(np.uint16)


def unstriped(offs):
    return offs[:16].T.reshape(-1).astype(np.int64)


def striped8(idx):
    return np.asarray(idx).reshape(8, -1, 16).transpose(0, 2, 1).reshape(128, -1).astype(np.uint16)


def unstriped8(offs):
    return offs.reshape(8, 16, -1).transpose(0, 2, 1).reshape(8, -1).astype(np.int64)


def pick8(x, idx, run):
    r = np.arange(len(x))
    return x[r[:, None], idx[r % (8 * run) // run]]


E2M1 = np.array([0.0, 0.5, 1.0, 1.5, 2.0, 3.0, 4.0, 6.0, -0.0, -0.5, -1.0, -1.5, -2.0, -3.0, -4.0, -6.0])


def pack_weight(w, fmt):
    k, n = w.shape
    w = f64(np.asarray(w, np.float32).astype(ml_dtypes.bfloat16)).reshape(k // 32, 32, n)
    amax = np.abs(w).max(1)
    if fmt == "e4m3":
        byte = np.frexp(amax)[1] - 1 + 127 - 7
    else:
        mant, ex = np.frexp(amax / 6.0)
        byte = np.where(mant > 0.5, ex, ex - 1) + 127
    byte = np.clip(np.where(amax > 0, byte, 1), 1, 254)
    scaled = (w * np.exp2(127.0 - byte)[:, None, :]).reshape(k, n).astype(np.float32)
    by_word = np.ascontiguousarray(scaled.reshape(k // 512, 128, 4, n).transpose(0, 1, 3, 2))
    if fmt == "e4m3":
        words = by_word.astype(ml_dtypes.float8_e4m3fn).view(np.uint8)
    else:
        c = by_word.astype(ml_dtypes.float4_e2m1fn).view(np.uint8) & 0xF
        words = (c[..., 0::2] | (c[..., 1::2] << 4)).reshape(k // 512, 128, 2 * n)
    return np.ascontiguousarray(words), np.ascontiguousarray(byte.astype(np.uint8).reshape(k // 512, 16, n))


def unpack_weight(words, scales, fmt):
    g, _, n = scales.shape
    words = np.ascontiguousarray(words).reshape(g, 128, n, -1)
    if fmt == "e4m3":
        vals = words.view(ml_dtypes.float8_e4m3fn).astype(np.float64)
    else:
        nib = np.empty((g, 128, n, 4), np.uint8)
        nib[..., 0::2] = words & 0xF
        nib[..., 1::2] = words >> 4
        vals = E2M1[nib]
    vals = vals * np.repeat(np.exp2(scales.astype(np.float64) - 127.0), 8, axis=1)[..., None]
    return vals.transpose(0, 1, 3, 2).reshape(g * 512, n)


K, J, R, T, O, S, N, Z, V, U = 512, 1024, 512, 2048, 256, 512, 256, 512, 1024, 128


def setup_inputs():
    n = np.random.standard_normal
    idx = np.stack([np.random.permutation(T)[:J] for _ in range(8)])
    idx2 = np.stack([np.random.permutation(J)[:S] for _ in range(8)])
    idx3 = np.stack([np.random.permutation(S)[:O] for _ in range(8)])
    idx4 = np.random.permutation(S)[:O]
    idx5 = np.random.permutation(V)[:O]
    idx6 = np.stack([np.random.permutation(O)[:U] for _ in range(8)])
    idx7 = np.stack([np.random.permutation(O)[:U] for _ in range(8)])
    fk = mx_kscale(K)
    fr = mx_kscale(R)
    fz = mx_kscale(Z)
    wp = pack_weight(n((K, R)) * 1 / np.sqrt(K) / fk[:, None] * fr, "e4m3")
    wbp = pack_weight(n((R, N)) * 1 / np.sqrt(R) / fr[:, None], "e2m1")
    xrp = pack_weight(n((Z, V)) / fz[:, None], "e4m3")
    wsp = pack_weight(n((Z, N)) * 1 / np.sqrt(Z) * fz[:, None], "e4m3")
    return {
        "ta": (np.random.randint(-7, 8, (K, T)).astype(np.float64)).astype(np.float32),
        "ga": ((np.random.randint(8, 25, (K, 1)) / 64.0) * fk[:, None]).astype(np.float32),
        "w_words": wp[0],
        "w_scales": wp[1],
        "sa": (np.random.uniform(0.5, 1.6, (R, 1))).astype(np.float32),
        "sb": (np.random.uniform(0.5, 1.6, (R, 1))).astype(np.float32),
        "sd": (np.random.uniform(0.5, 1.6, (R, 1))).astype(np.float32),
        "wb_words": wbp[0],
        "wb_scales": wbp[1],
        "xr_words": xrp[0],
        "xr_scales": xrp[1],
        "ws_words": wsp[0],
        "ws_scales": wsp[1],
        "so": (np.random.uniform(0.5, 1.6, (N, 1))).astype(np.float32),
        "sp": (np.random.uniform(0.5, 1.6, (N, 1))).astype(np.float32),
        "offs": striped8(idx),
        "offs2": striped8(idx2),
        "offs3": striped8(idx3),
        "offs4": striped(idx4),
        "offs5": striped(idx5),
        "offs6": striped8(idx6),
        "offs7": striped8(idx7),
    }


def reference(ta, ga, w_words, w_scales, sa, sb, sd, wb_words, wb_scales, xr_words, xr_scales, ws_words, ws_scales, so, sp, offs, offs2, offs3, offs4, offs5, offs6, offs7):
    idx = unstriped8(offs)
    idx2 = unstriped8(offs2)
    idx3 = unstriped8(offs3)
    idx4 = unstriped(offs4)
    idx5 = unstriped(offs5)
    idx6 = unstriped8(offs6)
    idx7 = unstriped8(offs7)
    wu = unpack_weight(w_words, w_scales, "e4m3")
    wbu = unpack_weight(wb_words, wb_scales, "e2m1")
    xru = unpack_weight(xr_words, xr_scales, "e4m3")
    wsu = unpack_weight(ws_words, ws_scales, "e4m3")
    xc = pick8(f64(ta), idx, 64) * f64(ga)
    xcq = mxq(xc, 0, "e4m3")
    a = wu.T @ xcq
    h1 = pick8(a, idx2, 64) * f64(sa)
    hid = np.abs(pick8(h1, idx3, 64) * f64(sb) - h1[:, idx4] * f64(sd))
    hidq = mxq(hid, 0, "e4m3")
    xridx5g = xru[:, idx5]
    p = wbu.T @ hidq + wsu.T @ xridx5g
    y = np.maximum(pick8(p, idx6, 16) * f64(so), pick8(p, idx7, 16) * f64(sp))
    return y

@@ -1,0 +1,258 @@
+from contextlib import ExitStack
+
+import concourse.mybir as mybir
+
+K, J, R, T, O, S, N, Z, V, U = 512, 1024, 512, 2048, 256, 512, 256, 512, 1024, 128
+FLOPS = 2 * K * R * J + 2 * R * N * O + 2 * Z * N * O
+
+F32 = mybir.dt.float32
+BF16 = mybir.dt.bfloat16
+I32 = mybir.dt.int32
+U32 = mybir.dt.uint32
+U16 = mybir.dt.uint16
+U8 = mybir.dt.uint8
+FP8X4 = mybir.dt.float8_e4m3fn_x4
+FP4X4 = mybir.dt.float4_e2m1fn_x4
+COPY = mybir.ActivationFunctionType.Copy
+ALU = mybir.AluOpType
+
+P = 128
+PACK = 4
+LIST_ROWS = 16
+HALF_J = J // 2
+PIECE_J = J // 4
+HALF_O = O // 2
+N_TILES = N // P
+
+
+def tile_picked_codes_plain_one_chain_reminder_grouppairs_kernel(
+    tc, ta, ga, w_words, w_scales, sa, sb, sd, wb_words, wb_scales, xr_words, xr_scales,
+    ws_words, ws_scales, so, sp, offs, offs2, offs3, offs4, offs5, offs6, offs7, out,
+):
+    nc = tc.nc
+
+    with ExitStack() as ctx:
+        keep = ctx.enter_context(tc.tile_pool(name="keep", bufs=1))
+        psum = ctx.enter_context(tc.psum_pool(name="psum", bufs=1))
+
+        def held(name, shape, dtype):
+            return keep.tile(shape, dtype, name=name, align_bytes=64)
+
+        def bank(index, width, name):
+            return psum.tile([P, width], F32, name=name, tag="bank%d" % index)
+
+        def load_list(name, src):
+            dst = held(name, list(src.shape), U16)
+            nc.sync.dma_start(dst[:], src)
+            return dst
+
+        def load_dealt_factor(name, src, queue):
+            dst = held(name, [P, PACK], F32)
+            queue.dma_start(dst[:], src.rearrange("(p t) one -> p (t one)", t=PACK))
+            return dst
+
+        def load_plain_factor(name, src):
+            dst = held(name, [P, N_TILES], F32)
+            with nc.allow_non_contiguous_dma(reason="one value a partition for each output tile"):
+                nc.sync.dma_start(dst[:], src.rearrange("(a p) one -> p (a one)", p=P))
+            return dst
+
+        def load_fp8_words(name, src):
+            dst = held(name, [P, src.shape[2]], U32)
+            nc.sync.dma_start(dst[:].bitcast(I32), src[0].rearrange("p n t -> p (n t)").bitcast(I32))
+            return dst
+
+        def cleared_scale_tile(name, width):
+            dst = held(name, [P, width], U8)
+            nc.vector.memset(dst[:].bitcast(I32), 0)
+            return dst
+
+        def load_scale_rows(dst, src):
+            for q in range(4):
+                nc.sync.dma_start(dst[32 * q : 32 * q + 4, :].bitcast(I32), src[0, 4 * q : 4 * q + 4, :].bitcast(I32))
+
+        def fetch_scaled(dst, window, offsets, first, count, factor):
+            cols = slice(first // LIST_ROWS, (first + count) // LIST_ROWS)
+            nc.scalar.activation(out=dst, in_=window[:].indirect(offsets[:, cols]), func=COPY, scale=factor)
+
+        w_sc_raw = cleared_scale_tile("w_sc_raw", R)
+        xr_sc = cleared_scale_tile("xr_sc", V)
+        ws_sc = cleared_scale_tile("ws_sc", N)
+        wb_sc = cleared_scale_tile("wb_sc", N)
+
+        list1 = load_list("list1", offs)
+        ga_sb = load_dealt_factor("ga_sb", ga, nc.scalar)
+        ta_dealt = ta.rearrange("(p t) c -> p t c", t=PACK)
+        ta_sb = []
+        for t in range(PACK):
+            if t == PACK - 1:
+                w_sc_rows = keep.tile([4, 4, R // 4], I32, name="w_sc_rows", align_bytes=64)
+                nc.sync.dma_start(w_sc_rows[:], w_scales[0].bitcast(I32).rearrange("(q i) n -> i q n", i=4))
+                w_raw = load_fp8_words("w_raw", w_words)
+            rows = held("ta%d" % t, [P, T], F32)
+            nc.sync.dma_start(rows[:], ta_dealt[:, t, :])
+            ta_sb.append(rows)
+        list2 = load_list("list2", offs2)
+        sa_sb = load_dealt_factor("sa_sb", sa, nc.sync)
+        list3 = load_list("list3", offs3)
+        list4 = load_list("list4", offs4)
+        sb_sb = load_dealt_factor("sb_sb", sb, nc.sync)
+        sd_sb = load_dealt_factor("sd_sb", sd, nc.sync)
+        list5 = load_list("list5", offs5)
+        xr_sb = load_fp8_words("xr_sb", xr_words)
+        load_scale_rows(xr_sc, xr_scales)
+        ws_sb = load_fp8_words("ws_sb", ws_words)
+        load_scale_rows(ws_sc, ws_scales)
+        wb_sb = held("wb_sb", [P, 2 * N], U8)
+        nc.sync.dma_start(wb_sb[:].bitcast(I32), wb_words[0].bitcast(I32))
+        load_scale_rows(wb_sc, wb_scales)
+        list6 = load_list("list6", offs6)
+        list7 = load_list("list7", offs7)
+        so_sb = load_plain_factor("so_sb", so)
+        sp_sb = load_plain_factor("sp_sb", sp)
+
+        xc_rows = [[held("xc_rows%d_%d" % (h, u), [P, 2, HALF_J], BF16) for u in range(2)] for h in range(2)]
+        xc_woven = [held("xc_woven%d" % c, [P, PIECE_J * PACK], BF16) for c in range(4)]
+        xc_words = [held("xc_words%d" % h, [P, HALF_J], U32) for h in range(2)]
+        xc_sc = [held("xc_sc%d" % h, [P, HALF_J], U8) for h in range(2)]
+        w_sb = held("w_sb", [P, R], U32)
+        w_sc = held("w_sc", [P, R], U8)
+
+        def weave_xc(h, u, c, move):
+            woven = xc_woven[2 * h + c][:].rearrange("p (j t) -> p j t", t=PACK)
+            src = xc_rows[h][u][:, :, c * PIECE_J : (c + 1) * PIECE_J]
+            move(out=woven[:, :, 2 * u : 2 * u + 2], in_=src.rearrange("p t j -> p j t"))
+
+        def quantize_xc(h, c):
+            cols = slice(c * PIECE_J, (c + 1) * PIECE_J)
+            nc.vector.quantize_mx(
+                out=xc_words[h][:, cols].bitcast(FP8X4), scales=xc_sc[h][:, cols], in_=xc_woven[2 * h + c][:]
+            )
+
+        a_sb = [held("a%d" % t, [P, J], F32) for t in range(PACK)]
+
+        def first_product(t, h, first, width, acc):
+            rows = slice(t * P, (t + 1) * P)
+            cols = slice(first, first + width)
+            nc.tensor.matmul_mx(
+                out=acc[:], lhsT=w_sb[:, rows].bitcast(FP8X4), lhsT_scale=w_sc[:, rows],
+                rhs=xc_words[h][:, cols].bitcast(FP8X4), rhs_scale=xc_sc[h][:, cols], start=True, stop=True,
+            )
+
+        for t in range(PACK):
+            for h in range(2):
+                fetch_scaled(xc_rows[h][t // 2][:, t % 2, :], ta_sb[t], list1, h * HALF_J, HALF_J, ga_sb[:, t : t + 1])
+                if t == 1:
+                    weave_xc(h, 0, 0, nc.vector.tensor_copy)
+                    weave_xc(h, 0, 1, nc.vector.tensor_copy)
+            if t == 2:
+                for q in range(4):
+                    nc.vector.tensor_copy(out=w_sc_raw[32 * q : 32 * q + 4, :].bitcast(I32), in_=w_sc_rows[:, q, :])
+                nc.vector.tensor_copy(
+                    out=w_sc[:].rearrange("p (t m) -> p t m", t=PACK), in_=w_sc_raw[:].rearrange("p (m t) -> p t m", t=PACK)
+                )
+                nc.vector.tensor_copy(
+                    out=w_sb[:].rearrange("p (t m) -> p t m", t=PACK), in_=w_raw[:].rearrange("p (m t) -> p t m", t=PACK)
+                )
+
+        weave_xc(0, 1, 0, nc.vector.tensor_copy)
+        weave_xc(0, 1, 1, nc.vector.tensor_copy)
+        quantize_xc(0, 0)
+        quantize_xc(0, 1)
+        weave_xc(1, 1, 0, nc.vector.tensor_copy)
+        weave_xc(1, 1, 1, nc.scalar.copy)
+        quantize_xc(1, 0)
+        quantize_xc(1, 1)
+
+        def product_piece(t, h, first, width, bank_index, move):
+            acc = bank(bank_index, width, "acc%d_%d_%d" % (t, h, first))
+            first_product(t, h, first, width, acc)
+            move(out=a_sb[t][:, h * HALF_J + first : h * HALF_J + first + width], in_=acc[:])
+
+        product_piece(0, 0, 0, HALF_J, 0, nc.scalar.copy)
+        product_piece(0, 1, 0, PIECE_J, 1, nc.scalar.copy)
+        product_piece(0, 1, PIECE_J, PIECE_J, 2, nc.scalar.copy)
+        for t in range(1, PACK):
+            for h in range(2):
+                product_piece(t, h, 0, HALF_J, 1 + 2 * (t % 2) + h, nc.vector.tensor_copy)
+
+        xg_words = held("xg_words", [P, O], U32)
+        xg_sc = held("xg_sc", [P, O], U8)
+        nc.vector.tensor_copy(out=xg_words[:], in_=xr_sb[:].indirect(list5[:]))
+        nc.vector.tensor_copy(out=xg_sc[:], in_=xr_sc[:].indirect(list5[:]))
+
+        p_acc = [[bank(5 + 2 * h + a if h + a < 2 else 0, HALF_O, "p_acc%d_%d" % (h, a)) for a in range(N_TILES)] for h in range(2)]
+        for h in range(2):
+            cols = slice(h * HALF_O, (h + 1) * HALF_O)
+            for a in range(N_TILES):
+                rows = slice(a * P, (a + 1) * P)
+                nc.tensor.matmul_mx(
+                    out=p_acc[h][a][:], lhsT=ws_sb[:, rows].bitcast(FP8X4), lhsT_scale=ws_sc[:, rows],
+                    rhs=xg_words[:, cols].bitcast(FP8X4), rhs_scale=xg_sc[:, cols], start=True, stop=False,
+                )
+
+        h1 = [held("h1_%d" % t, [P, S], F32) for t in range(PACK)]
+        left = [[held("left%d_%d" % (t, h), [P, HALF_O], F32) for h in range(2)] for t in range(PACK - 1, PACK)]
+        right = [[held("right%d_%d" % (t, h), [P, HALF_O], F32) for h in range(2)] for t in range(PACK - 1, PACK)]
+        left_whole = [held("left_whole%d" % t, [P, O], F32) for t in range(PACK - 1)]
+        right_whole = [held("right_whole%d" % t, [P, O], F32) for t in range(PACK - 1)]
+        diff = [[held("diff%d_%d" % (u, h), [P, 2, HALF_O], F32) for h in range(2)] for u in range(2)]
+        hid_woven = [held("hid_woven%d" % h, [P, HALF_O * PACK], BF16) for h in range(2)]
+        hid_words = [held("hid_words%d" % h, [P, HALF_O], U32) for h in range(2)]
+        hid_sc = [held("hid_sc%d" % h, [P, HALF_O], U8) for h in range(2)]
+        p_sb = [held("p%d" % a, [P, O], F32) for a in range(N_TILES)]
+
+        def seats(t):
+            fetch_scaled(h1[t][:], a_sb[t], list2, 0, S, sa_sb[:, t : t + 1])
+
+        def magnitudes(u, h):
+            woven = hid_woven[h][:].rearrange("p (o t) -> p o t", t=PACK)
+            d = diff[u][h][:].rearrange("p t o -> p o t")
+            nc.vector.scalar_tensor_tensor(
+                out=woven[:, :, 2 * u : 2 * u + 2], in0=d, scalar=-1.0, in1=d, op0=ALU.mult, op1=ALU.max
+            )
+
+        def places_whole(t):
+            fetch_scaled(left_whole[t][:], h1[t], list3, 0, O, sb_sb[:, t : t + 1])
+            fetch_scaled(right_whole[t][:], h1[t], list4, 0, O, sd_sb[:, t : t + 1])
+            for h in range(2):
+                cols = slice(h * HALF_O, (h + 1) * HALF_O)
+                nc.vector.tensor_tensor(
+                    out=diff[t // 2][h][:, t % 2, :], in0=left_whole[t][:, cols], in1=right_whole[t][:, cols], op=ALU.subtract
+                )
+
+        seats(0)
+        for t in range(PACK - 1):
+            seats(t + 1)
+            places_whole(t)
+            if t == 1:
+                magnitudes(0, 0)
+                magnitudes(0, 1)
+
+        last = PACK - 1
+        for h in range(2):
+            fetch_scaled(left[0][h][:], h1[last], list3, h * HALF_O, HALF_O, sb_sb[:, last : last + 1])
+            fetch_scaled(right[0][h][:], h1[last], list4, h * HALF_O, HALF_O, sd_sb[:, last : last + 1])
+            nc.vector.tensor_tensor(out=diff[1][h][:, 1, :], in0=left[0][h][:], in1=right[0][h][:], op=ALU.subtract)
+            magnitudes(1, h)
+            nc.vector.quantize_mx(out=hid_words[h][:].bitcast(FP8X4), scales=hid_sc[h][:], in_=hid_woven[h][:])
+            for a in range(N_TILES):
+                nc.tensor.matmul_mx(
+                    out=p_acc[h][a][:], lhsT=wb_sb[:, 2 * a * P : 2 * (a + 1) * P].bitcast(FP4X4),
+                    lhsT_scale=wb_sc[:, a * P : (a + 1) * P],
+                    rhs=hid_words[h][:].bitcast(FP8X4), rhs_scale=hid_sc[h][:], start=False, stop=True,
+                )
+        for h in range(2):
+            cols = slice(h * HALF_O, (h + 1) * HALF_O)
+            nc.scalar.copy(out=p_sb[0][:, cols], in_=p_acc[h][0][:])
+            other = nc.scalar.copy if h == 0 else nc.vector.tensor_copy
+            other(out=p_sb[1][:, cols], in_=p_acc[h][1][:])
+
+        for a in range(N_TILES):
+            first = held("first%d" % a, [P, U], F32)
+            second = held("second%d" % a, [P, U], F32)
+            larger = held("larger%d" % a, [P, U], F32)
+            fetch_scaled(first[:], p_sb[a], list6, 0, U, so_sb[:, a : a + 1])
+            fetch_scaled(second[:], p_sb[a], list7, 0, U, sp_sb[:, a : a + 1])
+            nc.vector.tensor_tensor(out=larger[:], in0=first[:], in1=second[:], op=ALU.max)
+            nc.sync.dma_start(out[a * P : (a + 1) * P, :], larger[:])

@@ -75,6 +75,11 @@ def tile_picked_codes_plain_one_chain_reminder_grouppairs_kernel(
             cols = slice(first // LIST_ROWS, (first + count) // LIST_ROWS)
             nc.scalar.activation(out=dst, in_=window[:].indirect(offsets[:, cols]), func=COPY, scale=factor)
 
+        warm_in = held("warm_in", [P, 1], F32)
+        warm_out = held("warm_out", [P, 1], F32)
+        nc.vector.memset(warm_in[:], 0.0)
+        nc.scalar.activation(out=warm_out[:], in_=warm_in[:], func=COPY)
+
         w_sc_raw = cleared_scale_tile("w_sc_raw", R)
         xr_sc = cleared_scale_tile("xr_sc", V)
         ws_sc = cleared_scale_tile("ws_sc", N)

@@ -71,6 +71,15 @@ def tile_picked_codes_plain_one_chain_reminder_grouppairs_kernel(
             for q in range(4):
                 nc.sync.dma_start(dst[32 * q : 32 * q + 4, :].bitcast(I32), src[0, 4 * q : 4 * q + 4, :].bitcast(I32))
 
+        def load_scale_stage(name, src):
+            stage = keep.tile([4, 4, src.shape[2] // 4], I32, name=name, align_bytes=64)
+            nc.sync.dma_start(stage[:], src[0].bitcast(I32).rearrange("(q i) n -> i q n", i=4))
+            return stage
+
+        def spread_scale_rows(dst, stage):
+            for q in range(4):
+                nc.vector.tensor_copy(out=dst[32 * q : 32 * q + 4, :].bitcast(I32), in_=stage[:, q, :])
+
         def fetch_scaled(dst, window, offsets, first, count, factor):
             cols = slice(first // LIST_ROWS, (first + count) // LIST_ROWS)
             nc.scalar.activation(out=dst, in_=window[:].indirect(offsets[:, cols]), func=COPY, scale=factor)
@@ -85,18 +94,18 @@ def tile_picked_codes_plain_one_chain_reminder_grouppairs_kernel(
         ws_sc = cleared_scale_tile("ws_sc", N)
         wb_sc = cleared_scale_tile("wb_sc", N)
 
-        list1 = load_list("list1", offs)
         ga_sb = load_dealt_factor("ga_sb", ga, nc.scalar)
         ta_dealt = ta.rearrange("(p t) c -> p t c", t=PACK)
         ta_sb = []
         for t in range(PACK):
             if t == PACK - 1:
-                w_sc_rows = keep.tile([4, 4, R // 4], I32, name="w_sc_rows", align_bytes=64)
-                nc.sync.dma_start(w_sc_rows[:], w_scales[0].bitcast(I32).rearrange("(q i) n -> i q n", i=4))
-                w_raw = load_fp8_words("w_raw", w_words)
+                w_sc_rows = load_scale_stage("w_sc_rows", w_scales)
             rows = held("ta%d" % t, [P, T], F32)
             nc.sync.dma_start(rows[:], ta_dealt[:, t, :])
             ta_sb.append(rows)
+            if t == 0:
+                list1 = load_list("list1", offs)
+        w_raw = load_fp8_words("w_raw", w_words)
         list2 = load_list("list2", offs2)
         sa_sb = load_dealt_factor("sa_sb", sa, nc.sync)
         list3 = load_list("list3", offs3)
@@ -105,7 +114,7 @@ def tile_picked_codes_plain_one_chain_reminder_grouppairs_kernel(
         sd_sb = load_dealt_factor("sd_sb", sd, nc.sync)
         list5 = load_list("list5", offs5)
         xr_sb = load_fp8_words("xr_sb", xr_words)
-        load_scale_rows(xr_sc, xr_scales)
+        xr_sc_rows = load_scale_stage("xr_sc_rows", xr_scales)
         ws_sb = load_fp8_words("ws_sb", ws_words)
         load_scale_rows(ws_sc, ws_scales)
         wb_sb = held("wb_sb", [P, 2 * N], U8)
@@ -116,77 +125,93 @@ def tile_picked_codes_plain_one_chain_reminder_grouppairs_kernel(
         so_sb = load_plain_factor("so_sb", so)
         sp_sb = load_plain_factor("sp_sb", sp)
 
-        xc_rows = [[held("xc_rows%d_%d" % (h, u), [P, 2, HALF_J], BF16) for u in range(2)] for h in range(2)]
-        xc_woven = [held("xc_woven%d" % c, [P, PIECE_J * PACK], BF16) for c in range(4)]
+        pieces = [(0, 256), (256, 256), (512, 256), (768, 128), (896, 128)]
+        xc_low = held("xc_low", [P, 2, J], BF16)
+        xc_high = [held("xc_high%d" % h, [P, 2, HALF_J], BF16) for h in range(2)]
+        xc_woven = [held("xc_woven%d" % c, [P, width * PACK], BF16) for c, (first, width) in enumerate(pieces)]
         xc_words = [held("xc_words%d" % h, [P, HALF_J], U32) for h in range(2)]
         xc_sc = [held("xc_sc%d" % h, [P, HALF_J], U8) for h in range(2)]
-        w_sb = held("w_sb", [P, R], U32)
+        w_sb = [held("w%d" % t, [P, P], U32) for t in range(PACK)]
         w_sc = held("w_sc", [P, R], U8)
-
-        def weave_xc(h, u, c, move):
-            woven = xc_woven[2 * h + c][:].rearrange("p (j t) -> p j t", t=PACK)
-            src = xc_rows[h][u][:, :, c * PIECE_J : (c + 1) * PIECE_J]
-            move(out=woven[:, :, 2 * u : 2 * u + 2], in_=src.rearrange("p t j -> p j t"))
-
-        def quantize_xc(h, c):
-            cols = slice(c * PIECE_J, (c + 1) * PIECE_J)
-            nc.vector.quantize_mx(
-                out=xc_words[h][:, cols].bitcast(FP8X4), scales=xc_sc[h][:, cols], in_=xc_woven[2 * h + c][:]
-            )
-
         a_sb = [held("a%d" % t, [P, J], F32) for t in range(PACK)]
 
-        def first_product(t, h, first, width, acc):
-            rows = slice(t * P, (t + 1) * P)
-            cols = slice(first, first + width)
+        def weave_low(c):
+            first, width = pieces[c]
+            woven = xc_woven[c][:].rearrange("p (j t) -> p j t", t=PACK)
+            nc.vector.tensor_copy(out=woven[:, :, 0:2], in_=xc_low[:, :, first : first + width].rearrange("p t j -> p j t"))
+
+        def weave_high(c, move):
+            first, width = pieces[c]
+            h, start = divmod(first, HALF_J)
+            woven = xc_woven[c][:].rearrange("p (j t) -> p j t", t=PACK)
+            move(out=woven[:, :, 2:4], in_=xc_high[h][:, :, start : start + width].rearrange("p t j -> p j t"))
+
+        def quantize_xc(c):
+            first, width = pieces[c]
+            h, start = divmod(first, HALF_J)
+            cols = slice(start, start + width)
+            nc.vector.quantize_mx(out=xc_words[h][:, cols].bitcast(FP8X4), scales=xc_sc[h][:, cols], in_=xc_woven[c][:])
+
+        def deal_w(t):
+            nc.vector.tensor_copy(out=w_sb[t][:], in_=w_raw[:].rearrange("p (m t) -> p t m", t=PACK)[:, t, :])
+
+        def first_product(t, first, width, acc):
+            h, start = divmod(first, HALF_J)
+            cols = slice(start, start + width)
             nc.tensor.matmul_mx(
-                out=acc[:], lhsT=w_sb[:, rows].bitcast(FP8X4), lhsT_scale=w_sc[:, rows],
+                out=acc, lhsT=w_sb[t][:].bitcast(FP8X4), lhsT_scale=w_sc[:, t * P : (t + 1) * P],
                 rhs=xc_words[h][:, cols].bitcast(FP8X4), rhs_scale=xc_sc[h][:, cols], start=True, stop=True,
             )
 
-        for t in range(PACK):
+        def product_piece(t, first, width, bank_index, move):
+            acc = bank(bank_index, width, "acc%d_%d" % (t, first))
+            first_product(t, first, width, acc[:])
+            move(out=a_sb[t][:, first : first + width], in_=acc[:])
+
+        for t in range(2):
+            fetch_scaled(xc_low[:, t, :], ta_sb[t], list1, 0, J, ga_sb[:, t : t + 1])
+        for c in range(len(pieces)):
+            weave_low(c)
+        spread_scale_rows(w_sc_raw, w_sc_rows)
+        nc.vector.tensor_copy(
+            out=w_sc[:].rearrange("p (t m) -> p t m", t=PACK), in_=w_sc_raw[:].rearrange("p (m t) -> p t m", t=PACK)
+        )
+        for t in range(2, PACK):
             for h in range(2):
-                fetch_scaled(xc_rows[h][t // 2][:, t % 2, :], ta_sb[t], list1, h * HALF_J, HALF_J, ga_sb[:, t : t + 1])
-                if t == 1:
-                    weave_xc(h, 0, 0, nc.vector.tensor_copy)
-                    weave_xc(h, 0, 1, nc.vector.tensor_copy)
-            if t == 2:
-                for q in range(4):
-                    nc.vector.tensor_copy(out=w_sc_raw[32 * q : 32 * q + 4, :].bitcast(I32), in_=w_sc_rows[:, q, :])
-                nc.vector.tensor_copy(
-                    out=w_sc[:].rearrange("p (t m) -> p t m", t=PACK), in_=w_sc_raw[:].rearrange("p (m t) -> p t m", t=PACK)
-                )
-                nc.vector.tensor_copy(
-                    out=w_sb[:].rearrange("p (t m) -> p t m", t=PACK), in_=w_raw[:].rearrange("p (m t) -> p t m", t=PACK)
-                )
+                fetch_scaled(xc_high[h][:, t - 2, :], ta_sb[t], list1, h * HALF_J, HALF_J, ga_sb[:, t : t + 1])
 
-        weave_xc(0, 1, 0, nc.vector.tensor_copy)
-        weave_xc(0, 1, 1, nc.vector.tensor_copy)
-        quantize_xc(0, 0)
-        quantize_xc(0, 1)
-        weave_xc(1, 1, 0, nc.vector.tensor_copy)
-        weave_xc(1, 1, 1, nc.scalar.copy)
-        quantize_xc(1, 0)
-        quantize_xc(1, 1)
+        deal_w(0)
+        weave_high(0, nc.vector.tensor_copy)
+        weave_high(1, nc.vector.tensor_copy)
+        quantize_xc(0)
+        quantize_xc(1)
+        weave_high(2, nc.vector.tensor_copy)
+        weave_high(3, nc.scalar.copy)
+        weave_high(4, nc.scalar.copy)
+        quantize_xc(3)
+        quantize_xc(2)
+        quantize_xc(4)
 
-        def product_piece(t, h, first, width, bank_index, move):
-            acc = bank(bank_index, width, "acc%d_%d_%d" % (t, h, first))
-            first_product(t, h, first, width, acc)
-            move(out=a_sb[t][:, h * HALF_J + first : h * HALF_J + first + width], in_=acc[:])
-
-        product_piece(0, 0, 0, HALF_J, 0, nc.scalar.copy)
-        product_piece(0, 1, 0, PIECE_J, 1, nc.scalar.copy)
-        product_piece(0, 1, PIECE_J, PIECE_J, 2, nc.scalar.copy)
+        acc_first = bank(0, HALF_J, "acc_first")
+        for c in range(2):
+            first, width = pieces[c]
+            first_product(0, first, width, acc_first[:, first : first + width])
+        nc.scalar.copy(out=a_sb[0][:, 0:HALF_J], in_=acc_first[:])
+        product_piece(0, *pieces[3], 1, nc.scalar.copy)
+        product_piece(0, *pieces[2], 2, nc.scalar.copy)
+        product_piece(0, *pieces[4], 3, nc.vector.tensor_copy)
         for t in range(1, PACK):
+            deal_w(t)
             for h in range(2):
-                product_piece(t, h, 0, HALF_J, 1 + 2 * (t % 2) + h, nc.vector.tensor_copy)
+                product_piece(t, h * HALF_J, HALF_J, (1 if t == 2 else 4) + h, nc.vector.tensor_copy)
 
         xg_words = held("xg_words", [P, O], U32)
         xg_sc = held("xg_sc", [P, O], U8)
+        spread_scale_rows(xr_sc, xr_sc_rows)
         nc.vector.tensor_copy(out=xg_words[:], in_=xr_sb[:].indirect(list5[:]))
         nc.vector.tensor_copy(out=xg_sc[:], in_=xr_sc[:].indirect(list5[:]))
 
-        p_acc = [[bank(5 + 2 * h + a if h + a < 2 else 0, HALF_O, "p_acc%d_%d" % (h, a)) for a in range(N_TILES)] for h in range(2)]
+        p_acc = [[bank((6, 7, 0, 3)[2 * h + a], HALF_O, "p_acc%d_%d" % (h, a)) for a in range(N_TILES)] for h in range(2)]
         for h in range(2):
             cols = slice(h * HALF_O, (h + 1) * HALF_O)
             for a in range(N_TILES):

from contextlib import ExitStack

import concourse.mybir as mybir

K, J, R, T, O, S, N, Z, V, U = 512, 1024, 512, 2048, 256, 512, 256, 512, 1024, 128
FLOPS = 2 * K * R * J + 2 * R * N * O + 2 * Z * N * O

F32 = mybir.dt.float32
BF16 = mybir.dt.bfloat16
I32 = mybir.dt.int32
U32 = mybir.dt.uint32
U16 = mybir.dt.uint16
U8 = mybir.dt.uint8
FP8X4 = mybir.dt.float8_e4m3fn_x4
FP4X4 = mybir.dt.float4_e2m1fn_x4
COPY = mybir.ActivationFunctionType.Copy
ALU = mybir.AluOpType

P = 128
PACK = 4
LIST_ROWS = 16
HALF_J = J // 2
PIECE_J = J // 4
HALF_O = O // 2
N_TILES = N // P


def tile_picked_codes_plain_one_chain_reminder_grouppairs_kernel(
    tc, ta, ga, w_words, w_scales, sa, sb, sd, wb_words, wb_scales, xr_words, xr_scales,
    ws_words, ws_scales, so, sp, offs, offs2, offs3, offs4, offs5, offs6, offs7, out,
):
    nc = tc.nc

    with ExitStack() as ctx:
        keep = ctx.enter_context(tc.tile_pool(name="keep", bufs=1))
        psum = ctx.enter_context(tc.psum_pool(name="psum", bufs=1))

        def held(name, shape, dtype):
            return keep.tile(shape, dtype, name=name, align_bytes=64)

        def bank(index, width, name):
            return psum.tile([P, width], F32, name=name, tag="bank%d" % index)

        def load_list(name, src):
            dst = held(name, list(src.shape), U16)
            nc.sync.dma_start(dst[:], src)
            return dst

        def load_dealt_factor(name, src, queue):
            dst = held(name, [P, PACK], F32)
            queue.dma_start(dst[:], src.rearrange("(p t) one -> p (t one)", t=PACK))
            return dst

        def load_plain_factor(name, src):
            dst = held(name, [P, N_TILES], F32)
            with nc.allow_non_contiguous_dma(reason="one value a partition for each output tile"):
                nc.sync.dma_start(dst[:], src.rearrange("(a p) one -> p (a one)", p=P))
            return dst

        def load_fp8_words(name, src):
            dst = held(name, [P, src.shape[2]], U32)
            nc.sync.dma_start(dst[:].bitcast(I32), src[0].rearrange("p n t -> p (n t)").bitcast(I32))
            return dst

        def cleared_scale_tile(name, width):
            dst = held(name, [P, width], U8)
            nc.vector.memset(dst[:].bitcast(I32), 0)
            return dst

        def load_scale_rows(dst, src):
            for q in range(4):
                nc.sync.dma_start(dst[32 * q : 32 * q + 4, :].bitcast(I32), src[0, 4 * q : 4 * q + 4, :].bitcast(I32))

        def load_scale_stage(name, src):
            stage = keep.tile([4, 4, src.shape[2] // 4], I32, name=name, align_bytes=64)
            nc.sync.dma_start(stage[:], src[0].bitcast(I32).rearrange("(q i) n -> i q n", i=4))
            return stage

        def spread_scale_rows(dst, stage):
            for q in range(4):
                nc.vector.tensor_copy(out=dst[32 * q : 32 * q + 4, :].bitcast(I32), in_=stage[:, q, :])

        def fetch_scaled(dst, window, offsets, first, count, factor):
            cols = slice(first // LIST_ROWS, (first + count) // LIST_ROWS)
            nc.scalar.activation(out=dst, in_=window[:].indirect(offsets[:, cols]), func=COPY, scale=factor)

        warm_in = held("warm_in", [P, 1], F32)
        warm_out = held("warm_out", [P, 1], F32)
        nc.vector.memset(warm_in[:], 0.0)
        nc.scalar.activation(out=warm_out[:], in_=warm_in[:], func=COPY)

        w_sc_raw = cleared_scale_tile("w_sc_raw", R)
        xr_sc = cleared_scale_tile("xr_sc", V)
        ws_sc = cleared_scale_tile("ws_sc", N)
        wb_sc = cleared_scale_tile("wb_sc", N)

        ga_sb = load_dealt_factor("ga_sb", ga, nc.scalar)
        ta_dealt = ta.rearrange("(p t) c -> p t c", t=PACK)
        ta_sb = []
        for t in range(PACK):
            if t == PACK - 1:
                w_sc_rows = load_scale_stage("w_sc_rows", w_scales)
            rows = held("ta%d" % t, [P, T], F32)
            nc.sync.dma_start(rows[:], ta_dealt[:, t, :])
            ta_sb.append(rows)
            if t == 0:
                list1 = load_list("list1", offs)
        w_raw = load_fp8_words("w_raw", w_words)
        list2 = load_list("list2", offs2)
        sa_sb = load_dealt_factor("sa_sb", sa, nc.sync)
        list3 = load_list("list3", offs3)
        list4 = load_list("list4", offs4)
        sb_sb = load_dealt_factor("sb_sb", sb, nc.sync)
        sd_sb = load_dealt_factor("sd_sb", sd, nc.sync)
        list5 = load_list("list5", offs5)
        xr_sb = load_fp8_words("xr_sb", xr_words)
        xr_sc_rows = load_scale_stage("xr_sc_rows", xr_scales)
        ws_sb = load_fp8_words("ws_sb", ws_words)
        load_scale_rows(ws_sc, ws_scales)
        wb_sb = held("wb_sb", [P, 2 * N], U8)
        nc.sync.dma_start(wb_sb[:].bitcast(I32), wb_words[0].bitcast(I32))
        load_scale_rows(wb_sc, wb_scales)
        list6 = load_list("list6", offs6)
        list7 = load_list("list7", offs7)
        so_sb = load_plain_factor("so_sb", so)
        sp_sb = load_plain_factor("sp_sb", sp)

        pieces = [(0, 256), (256, 256), (512, 256), (768, 128), (896, 128)]
        xc_low = held("xc_low", [P, 2, J], BF16)
        xc_high = [held("xc_high%d" % h, [P, 2, HALF_J], BF16) for h in range(2)]
        xc_woven = [held("xc_woven%d" % c, [P, width * PACK], BF16) for c, (first, width) in enumerate(pieces)]
        xc_words = [held("xc_words%d" % h, [P, HALF_J], U32) for h in range(2)]
        xc_sc = [held("xc_sc%d" % h, [P, HALF_J], U8) for h in range(2)]
        w_sb = [held("w%d" % t, [P, P], U32) for t in range(PACK)]
        w_sc = held("w_sc", [P, R], U8)
        a_sb = [held("a%d" % t, [P, J], F32) for t in range(PACK)]

        def weave_low(c):
            first, width = pieces[c]
            woven = xc_woven[c][:].rearrange("p (j t) -> p j t", t=PACK)
            nc.vector.tensor_copy(out=woven[:, :, 0:2], in_=xc_low[:, :, first : first + width].rearrange("p t j -> p j t"))

        def weave_high(c, move):
            first, width = pieces[c]
            h, start = divmod(first, HALF_J)
            woven = xc_woven[c][:].rearrange("p (j t) -> p j t", t=PACK)
            move(out=woven[:, :, 2:4], in_=xc_high[h][:, :, start : start + width].rearrange("p t j -> p j t"))

        def quantize_xc(c):
            first, width = pieces[c]
            h, start = divmod(first, HALF_J)
            cols = slice(start, start + width)
            nc.vector.quantize_mx(out=xc_words[h][:, cols].bitcast(FP8X4), scales=xc_sc[h][:, cols], in_=xc_woven[c][:])

        def deal_w(t):
            nc.vector.tensor_copy(out=w_sb[t][:], in_=w_raw[:].rearrange("p (m t) -> p t m", t=PACK)[:, t, :])

        def first_product(t, first, width, acc):
            h, start = divmod(first, HALF_J)
            cols = slice(start, start + width)
            nc.tensor.matmul_mx(
                out=acc, lhsT=w_sb[t][:].bitcast(FP8X4), lhsT_scale=w_sc[:, t * P : (t + 1) * P],
                rhs=xc_words[h][:, cols].bitcast(FP8X4), rhs_scale=xc_sc[h][:, cols], start=True, stop=True,
            )

        def product_piece(t, first, width, bank_index, move):
            acc = bank(bank_index, width, "acc%d_%d" % (t, first))
            first_product(t, first, width, acc[:])
            move(out=a_sb[t][:, first : first + width], in_=acc[:])

        for t in range(2):
            fetch_scaled(xc_low[:, t, :], ta_sb[t], list1, 0, J, ga_sb[:, t : t + 1])
        for c in range(len(pieces)):
            weave_low(c)
        spread_scale_rows(w_sc_raw, w_sc_rows)
        nc.vector.tensor_copy(
            out=w_sc[:].rearrange("p (t m) -> p t m", t=PACK), in_=w_sc_raw[:].rearrange("p (m t) -> p t m", t=PACK)
        )
        for t in range(2, PACK):
            for h in range(2):
                fetch_scaled(xc_high[h][:, t - 2, :], ta_sb[t], list1, h * HALF_J, HALF_J, ga_sb[:, t : t + 1])

        deal_w(0)
        weave_high(0, nc.vector.tensor_copy)
        weave_high(1, nc.vector.tensor_copy)
        quantize_xc(0)
        quantize_xc(1)
        weave_high(2, nc.vector.tensor_copy)
        weave_high(3, nc.scalar.copy)
        weave_high(4, nc.scalar.copy)
        quantize_xc(3)
        quantize_xc(2)
        quantize_xc(4)

        acc_first = bank(0, HALF_J, "acc_first")
        for c in range(2):
            first, width = pieces[c]
            first_product(0, first, width, acc_first[:, first : first + width])
        nc.scalar.copy(out=a_sb[0][:, 0:HALF_J], in_=acc_first[:])
        product_piece(0, *pieces[3], 1, nc.scalar.copy)
        product_piece(0, *pieces[2], 2, nc.scalar.copy)
        product_piece(0, *pieces[4], 3, nc.vector.tensor_copy)
        for t in range(1, PACK):
            deal_w(t)
            for h in range(2):
                product_piece(t, h * HALF_J, HALF_J, (1 if t == 2 else 4) + h, nc.vector.tensor_copy)

        xg_words = held("xg_words", [P, O], U32)
        xg_sc = held("xg_sc", [P, O], U8)
        spread_scale_rows(xr_sc, xr_sc_rows)
        nc.vector.tensor_copy(out=xg_words[:], in_=xr_sb[:].indirect(list5[:]))
        nc.vector.tensor_copy(out=xg_sc[:], in_=xr_sc[:].indirect(list5[:]))

        p_acc = [[bank((6, 7, 0, 3)[2 * h + a], HALF_O, "p_acc%d_%d" % (h, a)) for a in range(N_TILES)] for h in range(2)]
        for h in range(2):
            cols = slice(h * HALF_O, (h + 1) * HALF_O)
            for a in range(N_TILES):
                rows = slice(a * P, (a + 1) * P)
                nc.tensor.matmul_mx(
                    out=p_acc[h][a][:], lhsT=ws_sb[:, rows].bitcast(FP8X4), lhsT_scale=ws_sc[:, rows],
                    rhs=xg_words[:, cols].bitcast(FP8X4), rhs_scale=xg_sc[:, cols], start=True, stop=False,
                )

        h1 = [held("h1_%d" % t, [P, S], F32) for t in range(PACK)]
        left = [[held("left%d_%d" % (t, h), [P, HALF_O], F32) for h in range(2)] for t in range(PACK - 1, PACK)]
        right = [[held("right%d_%d" % (t, h), [P, HALF_O], F32) for h in range(2)] for t in range(PACK - 1, PACK)]
        left_whole = [held("left_whole%d" % t, [P, O], F32) for t in range(PACK - 1)]
        right_whole = [held("right_whole%d" % t, [P, O], F32) for t in range(PACK - 1)]
        diff = [[held("diff%d_%d" % (u, h), [P, 2, HALF_O], F32) for h in range(2)] for u in range(2)]
        hid_woven = [held("hid_woven%d" % h, [P, HALF_O * PACK], BF16) for h in range(2)]
        hid_words = [held("hid_words%d" % h, [P, HALF_O], U32) for h in range(2)]
        hid_sc = [held("hid_sc%d" % h, [P, HALF_O], U8) for h in range(2)]
        p_sb = [held("p%d" % a, [P, O], F32) for a in range(N_TILES)]

        def seats(t):
            fetch_scaled(h1[t][:], a_sb[t], list2, 0, S, sa_sb[:, t : t + 1])

        def magnitudes(u, h):
            woven = hid_woven[h][:].rearrange("p (o t) -> p o t", t=PACK)
            d = diff[u][h][:].rearrange("p t o -> p o t")
            nc.vector.scalar_tensor_tensor(
                out=woven[:, :, 2 * u : 2 * u + 2], in0=d, scalar=-1.0, in1=d, op0=ALU.mult, op1=ALU.max
            )

        def places_whole(t):
            fetch_scaled(left_whole[t][:], h1[t], list3, 0, O, sb_sb[:, t : t + 1])
            fetch_scaled(right_whole[t][:], h1[t], list4, 0, O, sd_sb[:, t : t + 1])
            for h in range(2):
                cols = slice(h * HALF_O, (h + 1) * HALF_O)
                nc.vector.tensor_tensor(
                    out=diff[t // 2][h][:, t % 2, :], in0=left_whole[t][:, cols], in1=right_whole[t][:, cols], op=ALU.subtract
                )

        seats(0)
        for t in range(PACK - 1):
            seats(t + 1)
            places_whole(t)
            if t == 1:
                magnitudes(0, 0)
                magnitudes(0, 1)

        last = PACK - 1
        for h in range(2):
            fetch_scaled(left[0][h][:], h1[last], list3, h * HALF_O, HALF_O, sb_sb[:, last : last + 1])
            fetch_scaled(right[0][h][:], h1[last], list4, h * HALF_O, HALF_O, sd_sb[:, last : last + 1])
            nc.vector.tensor_tensor(out=diff[1][h][:, 1, :], in0=left[0][h][:], in1=right[0][h][:], op=ALU.subtract)
            magnitudes(1, h)
            nc.vector.quantize_mx(out=hid_words[h][:].bitcast(FP8X4), scales=hid_sc[h][:], in_=hid_woven[h][:])
            for a in range(N_TILES):
                nc.tensor.matmul_mx(
                    out=p_acc[h][a][:], lhsT=wb_sb[:, 2 * a * P : 2 * (a + 1) * P].bitcast(FP4X4),
                    lhsT_scale=wb_sc[:, a * P : (a + 1) * P],
                    rhs=hid_words[h][:].bitcast(FP8X4), rhs_scale=hid_sc[h][:], start=False, stop=True,
                )
        for h in range(2):
            cols = slice(h * HALF_O, (h + 1) * HALF_O)
            nc.scalar.copy(out=p_sb[0][:, cols], in_=p_acc[h][0][:])
            other = nc.scalar.copy if h == 0 else nc.vector.tensor_copy
            other(out=p_sb[1][:, cols], in_=p_acc[h][1][:])

        for a in range(N_TILES):
            first = held("first%d" % a, [P, U], F32)
            second = held("second%d" % a, [P, U], F32)
            larger = held("larger%d" % a, [P, U], F32)
            fetch_scaled(first[:], p_sb[a], list6, 0, U, so_sb[:, a : a + 1])
            fetch_scaled(second[:], p_sb[a], list7, 0, U, sp_sb[:, a : a + 1])
            nc.vector.tensor_tensor(out=larger[:], in0=first[:], in1=second[:], op=ALU.max)
            nc.sync.dma_start(out[a * P : (a + 1) * P, :], larger[:])
